import numpy as np
import ml_dtypes


def mxq(x, axis, fmt="e4m3"):
    dtype, down = {"e4m3": (ml_dtypes.float8_e4m3fn, 7), "e5m2": (ml_dtypes.float8_e5m2, 14)}[fmt]
    v = np.moveaxis(np.asarray(x, np.float32).astype(ml_dtypes.bfloat16).astype(np.float64), axis, -1)
    blocks = v.reshape(v.shape[:-1] + (-1, 32))
    amax = np.abs(blocks).max(-1, keepdims=True)
    byte = np.maximum(np.where(amax > 0, np.frexp(amax)[1] - 1 + 127, 0) - down, 1)
    scale = np.exp2(byte - 127.0)
    codes = (blocks / scale).astype(np.float32).astype(dtype).astype(np.float64)
    return np.moveaxis((codes * scale).reshape(v.shape), -1, axis)


WIDE = False


def mx_kscale(k, group=512):
    if not WIDE:
        return np.ones(k)
    levels = np.array([10, -10, 5, -5, 0])
    if group != 512:
        return np.exp2(np.random.permutation(np.resize(levels, k // group))).repeat(group)
    if k % 512:
        return np.exp2(np.random.permutation(np.resize(levels, k // 32))).repeat(32)
    a = np.empty((k // 512, 16))
    for p in range(k // 512):
        a[p, :8] = np.random.permutation(np.resize(levels, 8))
        for g in range(8):
            far = levels[np.abs(levels - a[p, g]) >= 10]
            a[p, g + 8] = far[np.random.randint(len(far))]
    return np.exp2(a.ravel()).repeat(32)


def f64(x):
    return np.asarray(x).astype(np.float64)


def striped(idx):
    return np.tile(np.asarray(idx).reshape(-1, 16).T, (8, 1)).astype(np.uint16)


def unstriped(offs):
    return offs[:16].T.reshape(-1).astype(np.int64)


H, KV, D, NQ, N = 4, 1, 256, 512, 512


def setup_inputs():
    n = np.random.standard_normal
    s = mx_kscale(D, 0)[:, None]
    u = mx_kscale(N)
    t = np.random.uniform(0.5, 2.0, N) * u
    v = n((KV, N, 128))
    return {
        "qT": (n((H, D, NQ)) * s * (0.70 / np.sqrt(D))).astype(np.float32),
        "kT": (n((KV, D, N)) / s).astype(np.float32),
        "t": t.reshape(N, 1).astype(np.float32),
        "v": (v / t[:, None]).astype(np.float32),
        "mask": (np.arange(N)[:, None] <= np.sort(np.random.randint(N // 4, N, NQ))[None, :]).astype(np.float32),
        "og": n((H, NQ, 128)).astype(np.float32),
    }


def reference(qT, kT, t, v, mask, og):
    a = np.repeat(mxq(f64(kT), 1, "e4m3"), H // KV, 0).transpose(0, 2, 1) @ mxq(f64(qT), 1, "e4m3")
    p = a / (1.0 + np.exp(-a))
    p = p * f64(mask)
    w = p * f64(t)
    y = mxq(w, 1, "e4m3").transpose(0, 2, 1) @ np.repeat(mxq(f64(v), 1, "e4m3"), H // KV, 0)
    y = y / 16.0
    y = y / (1.0 + np.exp(-f64(og)))
    return y

@@ -1,0 +1,315 @@
+from contextlib import ExitStack
+
+import concourse.mybir as mybir
+
+H, D, NQ, N, E = 4, 256, 512, 512, 128
+FLOPS = 2 * H * N * NQ * D + 2 * H * NQ * N * E
+
+F32 = mybir.dt.float32
+BF16 = mybir.dt.bfloat16
+U32 = mybir.dt.uint32
+U8 = mybir.dt.uint8
+FP8X4 = mybir.dt.float8_e4m3fn_x4
+ACT = mybir.ActivationFunctionType
+ALU = mybir.AluOpType
+
+P = 128
+PACK = 4
+ROWS = 64
+QB = 128
+RUN = 2
+
+
+def tile_rows_a_silu_mask_gate_kernel(tc, qT, kT, t, v, mask, og, out):
+    nc = tc.nc
+    with ExitStack() as ctx:
+        sb = ctx.enter_context(tc.tile_pool(name="sb", bufs=1))
+        ps = ctx.enter_context(tc.psum_pool(name="ps", bufs=1))
+        ctx.enter_context(tc.manual_schedule())
+
+        def sbt(name, shape, dtype):
+            return sb.tile(shape, dtype, name=name, align_bytes=64)
+
+        score_banks = [[ps.tile([P, PACK, QB], F32, name="s%d_%d" % (g, b)) for b in range(3)] for g in range(2)]
+        y_banks = [ps.tile([P, 2, 2, E], F32, name="y%d" % b) for b in range(2)]
+
+        k_raw = sbt("k_raw", [P, PACK, N], F32)
+        k_src = kT[0].rearrange("(p j) n -> p j n", j=PACK)
+        nc.sync.dma_start(out=k_raw[0:ROWS], in_=k_src)
+        nc.scalar.dma_start(out=k_raw[ROWS:P], in_=k_src)
+
+        q_src = qT.rearrange("h (p j) n -> (h p) j n", j=PACK)
+        m_src = mask.rearrange("(p r) q -> p r q", r=PACK)
+        q_raw, m_raw, og_raw = {}, {}, {}
+
+        def load_q(i):
+            pair, half = divmod(i, 2)
+            q_raw[i] = sbt("q_raw%d" % i, [P, PACK, 2 * QB], F32)
+            nc.sync.dma_start(out=q_raw[i][:], in_=q_src[P * pair : P * (pair + 1), :, 2 * QB * half : 2 * QB * (half + 1)])
+
+        def load_mask(half):
+            m_raw[half] = sbt("m_raw%d" % half, [P, PACK, 2 * QB], F32)
+            nc.sync.dma_start(out=m_raw[half][:], in_=m_src[:, :, 2 * QB * half : 2 * QB * (half + 1)])
+
+        def load_og(pair):
+            og_raw[pair] = sbt("og_raw%d" % pair, [P, 2 * 4, E], F32)
+            nc.sync.dma_start(out=og_raw[pair][:], in_=og[2 * pair : 2 * pair + 2].rearrange("h (c p) e -> p (h c) e", p=P))
+
+        t_sb = sbt("t_sb", [P, PACK], F32)
+        v_raw = sbt("v_raw", [P, PACK, E], F32)
+        load_q(0)
+        nc.sync.dma_start(out=t_sb[:], in_=t.rearrange("(p r) o -> p (r o)", r=PACK))
+        load_mask(0)
+        load_q(1)
+        load_mask(1)
+        nc.sync.dma_start(out=v_raw[:], in_=v[0].rearrange("(p r) e -> p r e", r=PACK))
+        load_q(2)
+        load_og(0)
+        load_q(3)
+        load_og(1)
+
+        zero_in = sbt("zero_in", [P, 1], F32)
+        zero = sbt("zero", [P, 1], F32)
+        nc.vector.memset(zero_in[:], 0.0)
+        nc.scalar.activation(out=zero[:], in_=zero_in[:], func=ACT.Silu)
+
+        def quantize(name, src, words):
+            codes = sbt(name + "_c", [P, words], U32)
+            scales = sbt(name + "_s", [P, words], U8)
+            nc.vector.quantize_mx(out=codes[:].bitcast(FP8X4), scales=scales[:], in_=src)
+            return codes, scales
+
+        def copy_on(engine, dst, src):
+            if engine == "vector":
+                nc.vector.tensor_copy(out=dst, in_=src)
+            else:
+                nc.scalar.copy(out=dst, in_=src)
+
+        k_bf, k_mx, q_bf, q_mx, mt, pw, w_bf, w_mx, th = {}, {}, {}, {}, {}, {}, {}, {}, {}
+
+        def cast_k(rr, engine):
+            k_bf[rr] = sbt("k_bf%d" % rr, [P, 2, P, PACK], BF16)
+            src = k_raw[:].rearrange("p j (s rr r) -> p rr s j r", rr=2, r=2)[:, rr]
+            copy_on(engine, k_bf[rr][:].rearrange("p r s j -> p s j r"), src)
+
+        def quant_k(rr):
+            k_mx[rr] = quantize("k%d" % rr, k_bf[rr][:].rearrange("p r s j -> p (r s j)"), 2 * P)
+
+        def cast_q(u, engine):
+            q_bf[u] = sbt("q_bf%d" % u, [P, QB, PACK], BF16)
+            src = q_raw[u // 2][:, :, QB * (u % 2) : QB * (u % 2 + 1)].rearrange("p j (m i) -> p m j i", i=RUN)
+            copy_on(engine, q_bf[u][:].rearrange("p (m i) j -> p m j i", i=RUN), src)
+
+        def quant_q(u):
+            q_mx[u] = quantize("q%d" % u, q_bf[u][:].rearrange("p n j -> p (n j)"), QB)
+
+        def make_mt(c):
+            mt[c] = sbt("mt%d" % c, [P, QB, PACK], F32)
+            src = m_raw[c // 2][:, :, QB * (c % 2) : QB * (c % 2 + 1)].rearrange("p r (m i) -> p m r i", i=RUN)
+            nc.vector.tensor_tensor(
+                out=mt[c][:].rearrange("p (m i) r -> p m r i", i=RUN),
+                in0=src,
+                in1=t_sb[:].unsqueeze(1).unsqueeze(3).to_broadcast([P, QB // RUN, PACK, RUN]),
+                op=ALU.mult,
+            )
+
+        def scores(u):
+            order = [(g, r) for g in range(2) for r in range(PACK)] if u == 0 else [(g, r) for r in range(PACK) for g in range(2)]
+            qc, qs = q_mx[u]
+            for g, r in order:
+                rows = slice(ROWS * g, ROWS * (g + 1))
+                cols = slice(P * (r % 2), P * (r % 2 + 1))
+                kc, ks = k_mx[r // 2]
+                nc.tensor.matmul_mx(
+                    out=score_banks[g][u % 3][:, r, :],
+                    lhsT=kc[rows, cols].bitcast(FP8X4),
+                    lhsT_scale=ks[rows, cols],
+                    rhs=qc[rows, :].bitcast(FP8X4),
+                    rhs_scale=qs[rows, :],
+                    start=True,
+                    stop=True,
+                )
+
+        def silu(u):
+            for g in range(2):
+                pw[u, g] = sbt("p%d_%d" % (u, g), [P, QB, PACK], F32) if u in (0, 7) else None
+            if u not in (0, 7):
+                both = sbt("p%d" % u, [P, 2, QB, PACK], F32)
+                pw[u] = both
+            for g in range(2):
+                dst = pw[u, g][:] if u in (0, 7) else pw[u][:, g]
+                nc.scalar.activation(out=dst, in_=score_banks[g][u % 3][:].rearrange("p r q -> p q r"), func=ACT.Silu, bias=zero[:])
+
+        def mult(u):
+            w_bf[u] = sbt("w%d" % u, [P, 2, QB * PACK], BF16)
+            nc.vector.tensor_tensor(
+                out=w_bf[u][:],
+                in0=pw[u][:].rearrange("p g q r -> p g (q r)"),
+                in1=mt[u % 4][:].rearrange("p q r -> p (q r)").unsqueeze(1).to_broadcast([P, 2, QB * PACK]),
+                op=ALU.mult,
+            )
+
+        def mult_head(u, g):
+            w_bf[u, g] = sbt("w%d_%d" % (u, g), [P, QB * PACK], BF16)
+            nc.vector.tensor_tensor(
+                out=w_bf[u, g][:],
+                in0=pw[u, g][:].rearrange("p q r -> p (q r)"),
+                in1=mt[u % 4][:].rearrange("p q r -> p (q r)"),
+                op=ALU.mult,
+            )
+
+        def quant_w(u):
+            codes, scales = quantize("wq%d" % u, w_bf[u][:].rearrange("p g x -> p (g x)"), 2 * QB)
+            for g in range(2):
+                w_mx[u, g] = (codes[:, QB * g : QB * (g + 1)], scales[:, QB * g : QB * (g + 1)])
+
+        def quant_w_head(u, g):
+            codes, scales = quantize("wq%d_%d" % (u, g), w_bf[u, g][:], QB)
+            w_mx[u, g] = (codes[:], scales[:])
+
+        v_bf = sbt("v_bf", [P, E, PACK], BF16)
+        v_mx = []
+
+        def cast_v():
+            nc.scalar.activation(
+                out=v_bf[:].rearrange("p (m i) r -> p m r i", i=RUN),
+                in_=v_raw[:].rearrange("p r (m i) -> p m r i", i=RUN),
+                func=ACT.Copy,
+                scale=1.0 / 32.0,
+            )
+
+        def quant_v():
+            v_mx.extend(quantize("v", v_bf[:].rearrange("p e r -> p (e r)"), E))
+
+        y_place = {0: (0, 0), 1: (0, 1), 2: (1, 0), 3: (1, 1), 4: (0, 0), 5: (0, 1), 6: (1, 0), 7: (0, 1)}
+
+        def pv(u, heads=(0, 1)):
+            b, c = y_place[u]
+            for g in heads:
+                wc, ws = w_mx[u, g]
+                nc.tensor.matmul_mx(
+                    out=y_banks[b][:, g, c, :],
+                    lhsT=wc.bitcast(FP8X4),
+                    lhsT_scale=ws,
+                    rhs=v_mx[0][:].bitcast(FP8X4),
+                    rhs_scale=v_mx[1][:],
+                    start=True,
+                    stop=True,
+                )
+
+        def tanh(i):
+            pair, half = divmod(i, 2)
+            th[i] = sbt("th%d" % i, [P, 2, 2 * E], F32)
+            src = og_raw[pair][:].rearrange("p (h c) e -> p h (c e)", h=2)[:, :, 2 * E * half : 2 * E * (half + 1)]
+            nc.scalar.activation(out=th[i][:], in_=src, func=ACT.Tanh, scale=0.5)
+
+        def gate(i):
+            pair, half = divmod(i, 2)
+            res = sbt("res%d" % i, [P, 2, 2, E], F32)
+            nc.vector.scalar_tensor_tensor(
+                out=res[:].rearrange("p h c e -> p (h c e)"),
+                in0=th[i][:].rearrange("p h x -> p (h x)"),
+                scalar=1.0,
+                in1=y_banks[i % 2][:].rearrange("p h c e -> p (h c e)"),
+                op0=ALU.add,
+                op1=ALU.mult,
+            )
+            for g in range(2):
+                dst = out[2 * pair + g].rearrange("(c p) e -> p c e", p=P)[:, 2 * half : 2 * half + 2, :]
+                nc.sync.dma_start(out=dst, in_=res[:, g])
+
+        def gate_unit(u):
+            pair, c = divmod(u, 4)
+            b, slot = y_place[u]
+            res = sbt("resu%d" % u, [P, 2, E], F32)
+            nc.vector.scalar_tensor_tensor(
+                out=res[:],
+                in0=th[u // 2][:, :, E * (u % 2) : E * (u % 2 + 1)],
+                scalar=1.0,
+                in1=y_banks[b][:, :, slot, :],
+                op0=ALU.add,
+                op1=ALU.mult,
+            )
+            dst = out[2 * pair : 2 * pair + 2, P * c : P * (c + 1), :].rearrange("h p e -> p h e")
+            nc.sync.dma_start(out=dst, in_=res[:])
+
+        cast_k(0, "vector")
+        cast_k(1, "scalar")
+        quant_k(0)
+        cast_q(0, "scalar")
+        quant_k(1)
+        cast_q(1, "vector")
+        quant_q(0)
+        quant_q(1)
+        scores(0)
+        scores(1)
+        make_mt(0)
+        make_mt(1)
+        silu(0)
+        mult_head(0, 0)
+        cast_q(2, "vector")
+        mult_head(0, 1)
+        silu(1)
+        quant_q(2)
+        scores(2)
+        quant_w_head(0, 0)
+        quant_w_head(0, 1)
+        cast_q(3, "scalar")
+        cast_v()
+        mult(1)
+        quant_q(3)
+        quant_v()
+        scores(3)
+        pv(0)
+        make_mt(2)
+        quant_w(1)
+        pv(1)
+        silu(2)
+        cast_q(4, "scalar")
+        mult(2)
+        quant_q(4)
+        scores(4)
+        make_mt(3)
+        quant_w(2)
+        pv(2)
+        silu(3)
+        cast_q(5, "scalar")
+        tanh(0)
+        mult(3)
+        quant_q(5)
+        scores(5)
+        gate(0)
+        quant_w(3)
+        pv(3)
+        silu(4)
+        cast_q(6, "scalar")
+        mult(4)
+        quant_q(6)
+        scores(6)
+        quant_w(4)
+        pv(4)
+        silu(5)
+        cast_q(7, "scalar")
+        tanh(1)
+        mult(5)
+        quant_q(7)
+        scores(7)
+        gate(1)
+        quant_w(5)
+        pv(5)
+        silu(6)
+        tanh(2)
+        mult(6)
+        gate(2)
+        quant_w(6)
+        pv(6)
+        silu(7)
+        tanh(3)
+        mult_head(7, 0)
+        mult_head(7, 1)
+        quant_w_head(7, 0)
+        pv(7, (0,))
+        quant_w_head(7, 1)
+        pv(7, (1,))
+        gate_unit(6)
+        gate_unit(7)

@@ -9,6 +9,7 @@ F32 = mybir.dt.float32
 BF16 = mybir.dt.bfloat16
 U32 = mybir.dt.uint32
 U8 = mybir.dt.uint8
+I32 = mybir.dt.int32
 FP8X4 = mybir.dt.float8_e4m3fn_x4
 ACT = mybir.ActivationFunctionType
 ALU = mybir.AluOpType
@@ -33,10 +34,8 @@ def tile_rows_a_silu_mask_gate_kernel(tc, qT, kT, t, v, mask, og, out):
         score_banks = [[ps.tile([P, PACK, QB], F32, name="s%d_%d" % (g, b)) for b in range(3)] for g in range(2)]
         y_banks = [ps.tile([P, 2, 2, E], F32, name="y%d" % b) for b in range(2)]
 
-        k_raw = sbt("k_raw", [P, PACK, N], F32)
-        k_src = kT[0].rearrange("(p j) n -> p j n", j=PACK)
-        nc.sync.dma_start(out=k_raw[0:ROWS], in_=k_src)
-        nc.scalar.dma_start(out=k_raw[ROWS:P], in_=k_src)
+        k_raw = sbt("k_raw", [ROWS, PACK, N], F32)
+        nc.sync.dma_start(out=k_raw[:], in_=kT[0].rearrange("(p j) n -> p j n", j=PACK))
 
         q_src = qT.rearrange("h (p j) n -> (h p) j n", j=PACK)
         m_src = mask.rearrange("(p r) q -> p r q", r=PACK)
@@ -60,13 +59,18 @@ def tile_rows_a_silu_mask_gate_kernel(tc, qT, kT, t, v, mask, og, out):
         load_q(0)
         nc.sync.dma_start(out=t_sb[:], in_=t.rearrange("(p r) o -> p (r o)", r=PACK))
         load_mask(0)
-        load_q(1)
-        load_mask(1)
-        nc.sync.dma_start(out=v_raw[:], in_=v[0].rearrange("(p r) e -> p r e", r=PACK))
-        load_q(2)
-        load_og(0)
-        load_q(3)
-        load_og(1)
+
+        def later_loads():
+            load_q(1)
+            load_q(2)
+            load_mask(1)
+            load_q(3)
+            nc.sync.dma_start(out=v_raw[:], in_=v[0].rearrange("(p r) e -> p r e", r=PACK))
+            load_og(0)
+            load_og(1)
+
+        k_tiles = [sbt("k_mx%d" % g, [P, N + N // 4], U32) for g in range(2)]
+        nc.vector.memset(k_tiles[0][0:ROWS, N:], 0)
 
         zero_in = sbt("zero_in", [P, 1], F32)
         zero = sbt("zero", [P, 1], F32)
@@ -85,87 +89,97 @@ def tile_rows_a_silu_mask_gate_kernel(tc, qT, kT, t, v, mask, og, out):
             else:
                 nc.scalar.copy(out=dst, in_=src)
 
-        k_bf, k_mx, q_bf, q_mx, mt, pw, w_bf, w_mx, th = {}, {}, {}, {}, {}, {}, {}, {}, {}
+        k_bf, q_bf, q_mx, mt, pw, w_bf, w_mx, th = {}, {}, {}, {}, {}, {}, {}, {}
+        k_codes = [k_tiles[g][:, 0:N] for g in range(2)]
+        k_scales = [k_tiles[g][:, N:].bitcast(U8) for g in range(2)]
 
         def cast_k(rr, engine):
-            k_bf[rr] = sbt("k_bf%d" % rr, [P, 2, P, PACK], BF16)
+            k_bf[rr] = sbt("k_bf%d" % rr, [ROWS, 2, P, PACK], BF16)
             src = k_raw[:].rearrange("p j (s rr r) -> p rr s j r", rr=2, r=2)[:, rr]
             copy_on(engine, k_bf[rr][:].rearrange("p r s j -> p s j r"), src)
 
-        def quant_k(rr):
-            k_mx[rr] = quantize("k%d" % rr, k_bf[rr][:].rearrange("p r s j -> p (r s j)"), 2 * P)
+        def quant_k(r):
+            cols = slice(P * r, P * (r + 1))
+            nc.vector.quantize_mx(
+                out=k_codes[0][0:ROWS, cols].bitcast(FP8X4),
+                scales=k_scales[0][0:ROWS, cols],
+                in_=k_bf[r // 2][:, r % 2].rearrange("p s j -> p (s j)"),
+            )
 
-        def cast_q(u, engine):
-            q_bf[u] = sbt("q_bf%d" % u, [P, QB, PACK], BF16)
-            src = q_raw[u // 2][:, :, QB * (u % 2) : QB * (u % 2 + 1)].rearrange("p j (m i) -> p m j i", i=RUN)
-            copy_on(engine, q_bf[u][:].rearrange("p (m i) j -> p m j i", i=RUN), src)
+        def copy_k():
+            nc.sync.dma_start(out=k_tiles[1][ROWS:P, :].bitcast(I32), in_=k_tiles[0][0:ROWS, :].bitcast(I32))
 
-        def quant_q(u):
-            q_mx[u] = quantize("q%d" % u, q_bf[u][:].rearrange("p n j -> p (n j)"), QB)
+        def cast_q(i, c0, c1, engine):
+            key = (i, c0) if i == 0 else i
+            if key not in q_bf:
+                q_bf[key] = sbt("q_bf%d_%d" % (i, c0), [P, QB * (1 if i == 0 else 2), PACK], BF16)
+            dst = q_bf[key][:] if i == 0 else q_bf[key][:, QB * c0 : QB * c1, :]
+            src = q_raw[i][:, :, QB * c0 : QB * c1].rearrange("p j (m i) -> p m j i", i=RUN)
+            copy_on(engine, dst.rearrange("p (m i) j -> p m j i", i=RUN), src)
 
-        def make_mt(c):
-            mt[c] = sbt("mt%d" % c, [P, QB, PACK], F32)
-            src = m_raw[c // 2][:, :, QB * (c % 2) : QB * (c % 2 + 1)].rearrange("p r (m i) -> p m r i", i=RUN)
+        def quant_q_block(c):
+            codes, scales = quantize("q0_%d" % c, q_bf[0, c][:].rearrange("p n j -> p (n j)"), QB)
+            q_mx[0, c] = (codes[:], scales[:])
+
+        def quant_q(i):
+            codes, scales = quantize("q%d" % i, q_bf[i][:].rearrange("p n j -> p (n j)"), 2 * QB)
+            for c in range(2):
+                q_mx[i, c] = (codes[:, QB * c : QB * (c + 1)], scales[:, QB * c : QB * (c + 1)])
+
+        def make_mt(half, c0, c1):
+            if half not in mt:
+                mt[half] = sbt("mt%d" % half, [P, 2 * QB, PACK], F32)
+            src = m_raw[half][:, :, QB * c0 : QB * c1].rearrange("p r (m i) -> p m r i", i=RUN)
             nc.vector.tensor_tensor(
-                out=mt[c][:].rearrange("p (m i) r -> p m r i", i=RUN),
+                out=mt[half][:, QB * c0 : QB * c1, :].rearrange("p (m i) r -> p m r i", i=RUN),
                 in0=src,
-                in1=t_sb[:].unsqueeze(1).unsqueeze(3).to_broadcast([P, QB // RUN, PACK, RUN]),
+                in1=t_sb[:].unsqueeze(1).unsqueeze(3).to_broadcast([P, QB * (c1 - c0) // RUN, PACK, RUN]),
                 op=ALU.mult,
             )
+
+        def bank(u, c):
+            return score_banks[u % 2][(2 * (u // 2) + c) % 3]
 
         def scores(u):
-            order = [(g, r) for g in range(2) for r in range(PACK)] if u == 0 else [(g, r) for r in range(PACK) for g in range(2)]
-            qc, qs = q_mx[u]
-            for g, r in order:
-                rows = slice(ROWS * g, ROWS * (g + 1))
-                cols = slice(P * (r % 2), P * (r % 2 + 1))
-                kc, ks = k_mx[r // 2]
-                nc.tensor.matmul_mx(
-                    out=score_banks[g][u % 3][:, r, :],
-                    lhsT=kc[rows, cols].bitcast(FP8X4),
-                    lhsT_scale=ks[rows, cols],
-                    rhs=qc[rows, :].bitcast(FP8X4),
-                    rhs_scale=qs[rows, :],
-                    start=True,
-                    stop=True,
-                )
+            g = u % 2
+            rows = slice(ROWS * g, ROWS * (g + 1))
+            for c in range(2):
+                qc, qs = q_mx[u // 2, c]
+                for r in range(PACK):
+                    cols = slice(P * r, P * (r + 1))
+                    nc.tensor.matmul_mx(
+                        out=bank(u, c)[:, r, :],
+                        lhsT=k_codes[g][rows, cols].bitcast(FP8X4),
+                        lhsT_scale=k_scales[g][rows, cols],
+                        rhs=qc[rows, :].bitcast(FP8X4),
+                        rhs_scale=qs[rows, :],
+                        start=True,
+                        stop=True,
+                    )
 
-        def silu(u):
-            for g in range(2):
-                pw[u, g] = sbt("p%d_%d" % (u, g), [P, QB, PACK], F32) if u in (0, 7) else None
-            if u not in (0, 7):
-                both = sbt("p%d" % u, [P, 2, QB, PACK], F32)
-                pw[u] = both
-            for g in range(2):
-                dst = pw[u, g][:] if u in (0, 7) else pw[u][:, g]
-                nc.scalar.activation(out=dst, in_=score_banks[g][u % 3][:].rearrange("p r q -> p q r"), func=ACT.Silu, bias=zero[:])
+        def silu(u, c):
+            if u not in pw:
+                pw[u] = sbt("p%d" % u, [P, 2 * QB, PACK], F32)
+            nc.scalar.activation(
+                out=pw[u][:, QB * c : QB * (c + 1), :], in_=bank(u, c)[:].rearrange("p r q -> p q r"), func=ACT.Silu, bias=zero[:]
+            )
 
-        def mult(u):
-            w_bf[u] = sbt("w%d" % u, [P, 2, QB * PACK], BF16)
+        def mult(u, c0, c1):
+            if u not in w_bf:
+                w_bf[u] = sbt("w%d" % u, [P, 2 * QB * PACK], BF16)
+            cols = slice(QB * PACK * c0, QB * PACK * c1)
             nc.vector.tensor_tensor(
-                out=w_bf[u][:],
-                in0=pw[u][:].rearrange("p g q r -> p g (q r)"),
-                in1=mt[u % 4][:].rearrange("p q r -> p (q r)").unsqueeze(1).to_broadcast([P, 2, QB * PACK]),
+                out=w_bf[u][:, cols],
+                in0=pw[u][:].rearrange("p q r -> p (q r)")[:, cols],
+                in1=mt[(u // 2) % 2][:].rearrange("p q r -> p (q r)")[:, cols],
                 op=ALU.mult,
             )
 
-        def mult_head(u, g):
-            w_bf[u, g] = sbt("w%d_%d" % (u, g), [P, QB * PACK], BF16)
-            nc.vector.tensor_tensor(
-                out=w_bf[u, g][:],
-                in0=pw[u, g][:].rearrange("p q r -> p (q r)"),
-                in1=mt[u % 4][:].rearrange("p q r -> p (q r)"),
-                op=ALU.mult,
-            )
-
-        def quant_w(u):
-            codes, scales = quantize("wq%d" % u, w_bf[u][:].rearrange("p g x -> p (g x)"), 2 * QB)
-            for g in range(2):
-                w_mx[u, g] = (codes[:, QB * g : QB * (g + 1)], scales[:, QB * g : QB * (g + 1)])
-
-        def quant_w_head(u, g):
-            codes, scales = quantize("wq%d_%d" % (u, g), w_bf[u, g][:], QB)
-            w_mx[u, g] = (codes[:], scales[:])
+        def quant_w(u, c0, c1):
+            codes, scales = quantize("wq%d_%d" % (u, c0), w_bf[u][:, QB * PACK * c0 : QB * PACK * c1], QB * (c1 - c0))
+            for c in range(c0, c1):
+                cols = slice(QB * (c - c0), QB * (c - c0 + 1))
+                w_mx[u, c] = (codes[:, cols], scales[:, cols])
 
         v_bf = sbt("v_bf", [P, E, PACK], BF16)
         v_mx = []
@@ -181,14 +195,13 @@ def tile_rows_a_silu_mask_gate_kernel(tc, qT, kT, t, v, mask, og, out):
         def quant_v():
             v_mx.extend(quantize("v", v_bf[:].rearrange("p e r -> p (e r)"), E))
 
-        y_place = {0: (0, 0), 1: (0, 1), 2: (1, 0), 3: (1, 1), 4: (0, 0), 5: (0, 1), 6: (1, 0), 7: (0, 1)}
+        y_bank_of = [0, 0, 1, 1, 0, 0, 1, 0]
 
-        def pv(u, heads=(0, 1)):
-            b, c = y_place[u]
-            for g in heads:
-                wc, ws = w_mx[u, g]
+        def pv(u, blocks=(0, 1)):
+            for c in blocks:
+                wc, ws = w_mx[u, c]
                 nc.tensor.matmul_mx(
-                    out=y_banks[b][:, g, c, :],
+                    out=y_banks[y_bank_of[u]][:, u % 2, c, :],
                     lhsT=wc.bitcast(FP8X4),
                     lhsT_scale=ws,
                     rhs=v_mx[0][:].bitcast(FP8X4),
@@ -219,97 +232,97 @@ def tile_rows_a_silu_mask_gate_kernel(tc, qT, kT, t, v, mask, og, out):
                 nc.sync.dma_start(out=dst, in_=res[:, g])
 
         def gate_unit(u):
-            pair, c = divmod(u, 4)
-            b, slot = y_place[u]
+            pair, half = divmod(u // 2, 2)
             res = sbt("resu%d" % u, [P, 2, E], F32)
             nc.vector.scalar_tensor_tensor(
-                out=res[:],
-                in0=th[u // 2][:, :, E * (u % 2) : E * (u % 2 + 1)],
+                out=res[:].rearrange("p c e -> p (c e)"),
+                in0=th[u // 2][:, u % 2, :],
                 scalar=1.0,
-                in1=y_banks[b][:, :, slot, :],
+                in1=y_banks[y_bank_of[u]][:, u % 2].rearrange("p c e -> p (c e)"),
                 op0=ALU.add,
                 op1=ALU.mult,
             )
-            dst = out[2 * pair : 2 * pair + 2, P * c : P * (c + 1), :].rearrange("h p e -> p h e")
+            dst = out[2 * pair + u % 2].rearrange("(c p) e -> p c e", p=P)[:, 2 * half : 2 * half + 2, :]
             nc.sync.dma_start(out=dst, in_=res[:])
 
         cast_k(0, "vector")
         cast_k(1, "scalar")
-        quant_k(0)
-        cast_q(0, "scalar")
-        quant_k(1)
-        cast_q(1, "vector")
-        quant_q(0)
-        quant_q(1)
+        for r in range(PACK):
+            quant_k(r)
+        copy_k()
+        later_loads()
+        cast_q(0, 0, 1, "scalar")
+        cast_q(0, 1, 2, "vector")
+        quant_q_block(0)
+        quant_q_block(1)
         scores(0)
         scores(1)
-        make_mt(0)
-        make_mt(1)
-        silu(0)
-        mult_head(0, 0)
-        cast_q(2, "vector")
-        mult_head(0, 1)
-        silu(1)
-        quant_q(2)
+        make_mt(0, 0, 1)
+        make_mt(0, 1, 2)
+        silu(0, 0)
+        silu(0, 1)
+        silu(1, 0)
+        cast_q(1, 0, 1, "scalar")
+        mult(0, 0, 1)
+        mult(0, 1, 2)
+        cast_q(1, 1, 2, "vector")
+        silu(1, 1)
+        quant_w(0, 0, 2)
+        quant_q(1)
         scores(2)
-        quant_w_head(0, 0)
-        quant_w_head(0, 1)
-        cast_q(3, "scalar")
-        cast_v()
-        mult(1)
-        quant_q(3)
-        quant_v()
         scores(3)
-        pv(0)
-        make_mt(2)
-        quant_w(1)
-        pv(1)
-        silu(2)
-        cast_q(4, "scalar")
-        mult(2)
-        quant_q(4)
+        cast_q(2, 0, 2, "scalar")
+        mult(1, 0, 2)
+        make_mt(1, 0, 2)
+        quant_w(1, 0, 2)
+        quant_q(2)
+        silu(2, 0)
+        silu(2, 1)
         scores(4)
-        make_mt(3)
-        quant_w(2)
-        pv(2)
-        silu(3)
-        cast_q(5, "scalar")
-        tanh(0)
-        mult(3)
-        quant_q(5)
+        silu(3, 0)
+        silu(3, 1)
         scores(5)
-        gate(0)
-        quant_w(3)
-        pv(3)
-        silu(4)
-        cast_q(6, "scalar")
-        mult(4)
-        quant_q(6)
+        mult(2, 0, 2)
+        cast_q(3, 0, 2, "scalar")
+        mult(3, 0, 2)
+        quant_w(2, 0, 2)
+        quant_q(3)
+        quant_w(3, 0, 2)
+        silu(4, 0)
+        silu(4, 1)
         scores(6)
-        quant_w(4)
-        pv(4)
-        silu(5)
-        cast_q(7, "scalar")
-        tanh(1)
-        mult(5)
-        quant_q(7)
+        cast_v()
+        mult(4, 0, 2)
+        quant_v()
+        quant_w(4, 0, 2)
+        for u in range(4):
+            pv(u)
+        silu(5, 0)
+        silu(5, 1)
+        tanh(0)
         scores(7)
-        gate(1)
-        quant_w(5)
+        mult(5, 0, 2)
+        gate(0)
+        pv(4)
+        quant_w(5, 0, 2)
         pv(5)
-        silu(6)
+        tanh(1)
+        silu(6, 0)
+        silu(6, 1)
         tanh(2)
-        mult(6)
+        gate(1)
+        mult(6, 0, 2)
         gate(2)
-        quant_w(6)
+        quant_w(6, 0, 2)
         pv(6)
-        silu(7)
+        silu(7, 0)
+        silu(7, 1)
         tanh(3)
-        mult_head(7, 0)
-        mult_head(7, 1)
-        quant_w_head(7, 0)
+        mult(7, 0, 1)
+        mult(7, 1, 2)
+        quant_w(7, 0, 1)
         pv(7, (0,))
-        quant_w_head(7, 1)
+        quant_w(7, 1, 2)
         pv(7, (1,))
         gate_unit(6)
         gate_unit(7)

@@ -34,8 +34,10 @@ def tile_rows_a_silu_mask_gate_kernel(tc, qT, kT, t, v, mask, og, out):
         score_banks = [[ps.tile([P, PACK, QB], F32, name="s%d_%d" % (g, b)) for b in range(3)] for g in range(2)]
         y_banks = [ps.tile([P, 2, 2, E], F32, name="y%d" % b) for b in range(2)]
 
-        k_raw = sbt("k_raw", [ROWS, PACK, N], F32)
-        nc.sync.dma_start(out=k_raw[:], in_=kT[0].rearrange("(p j) n -> p j n", j=PACK))
+        k_src = kT[0].rearrange("(p j) n -> p j n", j=PACK)
+        k_raw = [sbt("k_raw%d" % a, [ROWS, PACK, N // 2], F32) for a in range(2)]
+        for a in range(2):
+            nc.sync.dma_start(out=k_raw[a][:], in_=k_src[:, :, N // 2 * a : N // 2 * (a + 1)])
 
         q_src = qT.rearrange("h (p j) n -> (h p) j n", j=PACK)
         m_src = mask.rearrange("(p r) q -> p r q", r=PACK)
@@ -93,10 +95,11 @@ def tile_rows_a_silu_mask_gate_kernel(tc, qT, kT, t, v, mask, og, out):
         k_codes = [k_tiles[g][:, 0:N] for g in range(2)]
         k_scales = [k_tiles[g][:, N:].bitcast(U8) for g in range(2)]
 
-        def cast_k(rr, engine):
-            k_bf[rr] = sbt("k_bf%d" % rr, [ROWS, 2, P, PACK], BF16)
-            src = k_raw[:].rearrange("p j (s rr r) -> p rr s j r", rr=2, r=2)[:, rr]
-            copy_on(engine, k_bf[rr][:].rearrange("p r s j -> p s j r"), src)
+        def cast_k(a, rr, engine):
+            if rr not in k_bf:
+                k_bf[rr] = sbt("k_bf%d" % rr, [ROWS, 2, P, PACK], BF16)
+            src = k_raw[a][:].rearrange("p j (s rr r) -> p rr s j r", rr=2, r=2)[:, rr]
+            copy_on(engine, k_bf[rr][:, :, P // 2 * a : P // 2 * (a + 1), :].rearrange("p r s j -> p s j r"), src)
 
         def quant_k(r):
             cols = slice(P * r, P * (r + 1))
@@ -126,16 +129,12 @@ def tile_rows_a_silu_mask_gate_kernel(tc, qT, kT, t, v, mask, og, out):
             for c in range(2):
                 q_mx[i, c] = (codes[:, QB * c : QB * (c + 1)], scales[:, QB * c : QB * (c + 1)])
 
-        def make_mt(half, c0, c1):
-            if half not in mt:
-                mt[half] = sbt("mt%d" % half, [P, 2 * QB, PACK], F32)
-            src = m_raw[half][:, :, QB * c0 : QB * c1].rearrange("p r (m i) -> p m r i", i=RUN)
-            nc.vector.tensor_tensor(
-                out=mt[half][:, QB * c0 : QB * c1, :].rearrange("p (m i) r -> p m r i", i=RUN),
-                in0=src,
-                in1=t_sb[:].unsqueeze(1).unsqueeze(3).to_broadcast([P, QB * (c1 - c0) // RUN, PACK, RUN]),
-                op=ALU.mult,
-            )
+        def make_mt(half):
+            mt[half] = sbt("mt%d" % half, [P, PACK, 2 * QB], F32)
+            for r in range(PACK):
+                nc.vector.tensor_scalar(
+                    out=mt[half][:, r, :], in0=m_raw[half][:, r, :], scalar1=t_sb[:, r : r + 1], scalar2=None, op0=ALU.mult
+                )
 
         def bank(u, c):
             return score_banks[u % 2][(2 * (u // 2) + c) % 3]
@@ -159,19 +158,21 @@ def tile_rows_a_silu_mask_gate_kernel(tc, qT, kT, t, v, mask, og, out):
 
         def silu(u, c):
             if u not in pw:
-                pw[u] = sbt("p%d" % u, [P, 2 * QB, PACK], F32)
+                pw[u] = sbt("p%d" % u, [P, 2 * QB // RUN, PACK, RUN], F32)
             nc.scalar.activation(
-                out=pw[u][:, QB * c : QB * (c + 1), :], in_=bank(u, c)[:].rearrange("p r q -> p q r"), func=ACT.Silu, bias=zero[:]
+                out=pw[u][:, QB // RUN * c : QB // RUN * (c + 1)],
+                in_=bank(u, c)[:].rearrange("p r (m i) -> p m r i", i=RUN),
+                func=ACT.Silu,
+                bias=zero[:],
             )
 
         def mult(u, c0, c1):
             if u not in w_bf:
                 w_bf[u] = sbt("w%d" % u, [P, 2 * QB * PACK], BF16)
-            cols = slice(QB * PACK * c0, QB * PACK * c1)
             nc.vector.tensor_tensor(
-                out=w_bf[u][:, cols],
-                in0=pw[u][:].rearrange("p q r -> p (q r)")[:, cols],
-                in1=mt[(u // 2) % 2][:].rearrange("p q r -> p (q r)")[:, cols],
+                out=w_bf[u][:, QB * PACK * c0 : QB * PACK * c1].rearrange("p (m i r) -> p m r i", i=RUN, r=PACK),
+                in0=pw[u][:, QB // RUN * c0 : QB // RUN * c1],
+                in1=mt[(u // 2) % 2][:, :, QB * c0 : QB * c1].rearrange("p r (m i) -> p m r i", i=RUN),
                 op=ALU.mult,
             )
 
@@ -195,13 +196,14 @@ def tile_rows_a_silu_mask_gate_kernel(tc, qT, kT, t, v, mask, og, out):
         def quant_v():
             v_mx.extend(quantize("v", v_bf[:].rearrange("p e r -> p (e r)"), E))
 
-        y_bank_of = [0, 0, 1, 1, 0, 0, 1, 0]
+        y_place = [(0, 0), (1, 1), (1, 0), (0, 1), (0, 0), (1, 1), (1, 0), (0, 1)]
 
         def pv(u, blocks=(0, 1)):
+            b, slot = y_place[u]
             for c in blocks:
                 wc, ws = w_mx[u, c]
                 nc.tensor.matmul_mx(
-                    out=y_banks[y_bank_of[u]][:, u % 2, c, :],
+                    out=y_banks[b][:, slot, c, :],
                     lhsT=wc.bitcast(FP8X4),
                     lhsT_scale=ws,
                     rhs=v_mx[0][:].bitcast(FP8X4),
@@ -210,55 +212,49 @@ def tile_rows_a_silu_mask_gate_kernel(tc, qT, kT, t, v, mask, og, out):
                     stop=True,
                 )
 
-        def tanh(i):
-            pair, half = divmod(i, 2)
-            th[i] = sbt("th%d" % i, [P, 2, 2 * E], F32)
-            src = og_raw[pair][:].rearrange("p (h c) e -> p h (c e)", h=2)[:, :, 2 * E * half : 2 * E * (half + 1)]
-            nc.scalar.activation(out=th[i][:], in_=src, func=ACT.Tanh, scale=0.5)
+        def quarters(ap, which):
+            return ap.rearrange("p (a c) e -> p a (c e)", c=2)[:, which, :]
 
-        def gate(i):
-            pair, half = divmod(i, 2)
-            res = sbt("res%d" % i, [P, 2, 2, E], F32)
+        def tanh(pair, which):
+            if pair not in th:
+                th[pair] = sbt("th%d" % pair, [P, 8, E], F32)
+            nc.scalar.activation(out=quarters(th[pair][:], which), in_=quarters(og_raw[pair][:], which), func=ACT.Tanh, scale=0.5)
+
+        def gate(pair, which, b, slots):
+            n = len(range(4)[which])
+            res = sbt("res%d_%d" % (pair, which.start), [P, n, 2 * E], F32)
             nc.vector.scalar_tensor_tensor(
-                out=res[:].rearrange("p h c e -> p (h c e)"),
-                in0=th[i][:].rearrange("p h x -> p (h x)"),
+                out=res[:],
+                in0=quarters(th[pair][:], which),
                 scalar=1.0,
-                in1=y_banks[i % 2][:].rearrange("p h c e -> p (h c e)"),
+                in1=y_banks[b][:].rearrange("p a c e -> p a (c e)")[:, slots, :],
                 op0=ALU.add,
                 op1=ALU.mult,
             )
-            for g in range(2):
-                dst = out[2 * pair + g].rearrange("(c p) e -> p c e", p=P)[:, 2 * half : 2 * half + 2, :]
-                nc.sync.dma_start(out=dst, in_=res[:, g])
+            rows = out[2 * pair : 2 * pair + 2].rearrange("h (c p) e -> p (h c) e", p=P)
+            if which.step == 1:
+                nc.sync.dma_start(out=rows[:, 2 * which.start : 2 * which.stop, :], in_=res[:].rearrange("p a (c e) -> p (a c) e", c=2))
+            else:
+                for i, a in enumerate(range(4)[which]):
+                    nc.sync.dma_start(out=rows[:, 2 * a : 2 * a + 2, :], in_=res[:, i, :].rearrange("p (c e) -> p c e", c=2))
 
-        def gate_unit(u):
-            pair, half = divmod(u // 2, 2)
-            res = sbt("resu%d" % u, [P, 2, E], F32)
-            nc.vector.scalar_tensor_tensor(
-                out=res[:].rearrange("p c e -> p (c e)"),
-                in0=th[u // 2][:, u % 2, :],
-                scalar=1.0,
-                in1=y_banks[y_bank_of[u]][:, u % 2].rearrange("p c e -> p (c e)"),
-                op0=ALU.add,
-                op1=ALU.mult,
-            )
-            dst = out[2 * pair + u % 2].rearrange("(c p) e -> p c e", p=P)[:, 2 * half : 2 * half + 2, :]
-            nc.sync.dma_start(out=dst, in_=res[:])
+        outer, inner, first, last = slice(0, 4, 3), slice(1, 3, 1), slice(0, 1, 1), slice(3, 4, 1)
 
-        cast_k(0, "vector")
-        cast_k(1, "scalar")
+        cast_k(0, 0, "vector")
+        cast_k(0, 1, "vector")
+        cast_k(1, 0, "vector")
+        cast_k(1, 1, "scalar")
         for r in range(PACK):
             quant_k(r)
+        cast_q(0, 0, 1, "vector")
+        cast_q(0, 1, 2, "scalar")
         copy_k()
         later_loads()
-        cast_q(0, 0, 1, "scalar")
-        cast_q(0, 1, 2, "vector")
         quant_q_block(0)
         quant_q_block(1)
         scores(0)
         scores(1)
-        make_mt(0, 0, 1)
-        make_mt(0, 1, 2)
+        make_mt(0)
         silu(0, 0)
         silu(0, 1)
         silu(1, 0)
@@ -273,7 +269,7 @@ def tile_rows_a_silu_mask_gate_kernel(tc, qT, kT, t, v, mask, og, out):
         scores(3)
         cast_q(2, 0, 2, "scalar")
         mult(1, 0, 2)
-        make_mt(1, 0, 2)
+        make_mt(1)
         quant_w(1, 0, 2)
         quant_q(2)
         silu(2, 0)
@@ -299,30 +295,30 @@ def tile_rows_a_silu_mask_gate_kernel(tc, qT, kT, t, v, mask, og, out):
             pv(u)
         silu(5, 0)
         silu(5, 1)
-        tanh(0)
+        tanh(0, outer)
         scores(7)
         mult(5, 0, 2)
-        gate(0)
+        gate(0, outer, 0, slice(0, 2))
         pv(4)
         quant_w(5, 0, 2)
-        pv(5)
-        tanh(1)
+        tanh(0, inner)
         silu(6, 0)
         silu(6, 1)
-        tanh(2)
-        gate(1)
+        tanh(1, first)
+        gate(0, inner, 1, slice(0, 2))
+        pv(5)
         mult(6, 0, 2)
-        gate(2)
+        gate(1, first, 0, slice(0, 1))
         quant_w(6, 0, 2)
         pv(6)
         silu(7, 0)
         silu(7, 1)
-        tanh(3)
+        tanh(1, slice(1, 4, 1))
         mult(7, 0, 1)
         mult(7, 1, 2)
         quant_w(7, 0, 1)
         pv(7, (0,))
         quant_w(7, 1, 2)
         pv(7, (1,))
-        gate_unit(6)
-        gate_unit(7)
+        gate(1, inner, 1, slice(0, 2))
+        gate(1, last, 0, slice(1, 2))

@@ -2,323 +2,325 @@ from contextlib import ExitStack
 
 import concourse.mybir as mybir
 
-H, D, NQ, N, E = 4, 256, 512, 512, 128
-FLOPS = 2 * H * N * NQ * D + 2 * H * NQ * N * E
+HEADS, FEATURES, QUERIES, TOKENS, VALUES = 4, 256, 512, 512, 128
+FLOPS = 2 * HEADS * TOKENS * QUERIES * (FEATURES + VALUES)
 
 F32 = mybir.dt.float32
 BF16 = mybir.dt.bfloat16
+I32 = mybir.dt.int32
 U32 = mybir.dt.uint32
 U8 = mybir.dt.uint8
-I32 = mybir.dt.int32
 FP8X4 = mybir.dt.float8_e4m3fn_x4
 ACT = mybir.ActivationFunctionType
 ALU = mybir.AluOpType
 
 P = 128
 PACK = 4
-ROWS = 64
-QB = 128
+TILE_ROWS = FEATURES // PACK
+BLOCK = 128
+HALF = 2 * BLOCK
 RUN = 2
+SCORE_BANKS = 3
 
 
 def tile_rows_a_silu_mask_gate_kernel(tc, qT, kT, t, v, mask, og, out):
     nc = tc.nc
     with ExitStack() as ctx:
-        sb = ctx.enter_context(tc.tile_pool(name="sb", bufs=1))
-        ps = ctx.enter_context(tc.psum_pool(name="ps", bufs=1))
+        sbuf = ctx.enter_context(tc.tile_pool(name="sbuf", bufs=1))
+        psum = ctx.enter_context(tc.psum_pool(name="psum", bufs=1))
         ctx.enter_context(tc.manual_schedule())
 
-        def sbt(name, shape, dtype):
-            return sb.tile(shape, dtype, name=name, align_bytes=64)
+        def tile(name, shape, dtype):
+            return sbuf.tile(shape, dtype, name=name, align_bytes=64)
 
-        score_banks = [[ps.tile([P, PACK, QB], F32, name="s%d_%d" % (g, b)) for b in range(3)] for g in range(2)]
-        y_banks = [ps.tile([P, 2, 2, E], F32, name="y%d" % b) for b in range(2)]
+        score_banks = [
+            [psum.tile([P, PACK, BLOCK], F32, name="s%d_%d" % (g, b)) for b in range(SCORE_BANKS)] for g in range(2)
+        ]
+        y_banks = [psum.tile([P, 2, 2, VALUES], F32, name="y%d" % b) for b in range(2)]
 
         k_src = kT[0].rearrange("(p j) n -> p j n", j=PACK)
-        k_raw = [sbt("k_raw%d" % a, [ROWS, PACK, N // 2], F32) for a in range(2)]
-        for a in range(2):
-            nc.sync.dma_start(out=k_raw[a][:], in_=k_src[:, :, N // 2 * a : N // 2 * (a + 1)])
-
         q_src = qT.rearrange("h (p j) n -> (h p) j n", j=PACK)
-        m_src = mask.rearrange("(p r) q -> p r q", r=PACK)
-        q_raw, m_raw, og_raw = {}, {}, {}
+        mask_src = mask.rearrange("(s r) q -> s r q", r=PACK)
+        k_raw, q_raw, mask_raw, og_raw = {}, {}, {}, {}
 
-        def load_q(i):
-            pair, half = divmod(i, 2)
-            q_raw[i] = sbt("q_raw%d" % i, [P, PACK, 2 * QB], F32)
-            nc.sync.dma_start(out=q_raw[i][:], in_=q_src[P * pair : P * (pair + 1), :, 2 * QB * half : 2 * QB * (half + 1)])
+        def load_k(a):
+            k_raw[a] = tile("k_raw%d" % a, [TILE_ROWS, PACK, TOKENS // 2], F32)
+            nc.sync.dma_start(out=k_raw[a][:], in_=k_src[:, :, TOKENS // 2 * a : TOKENS // 2 * (a + 1)])
+
+        def load_q(chunk):
+            pair, half = divmod(chunk, 2)
+            q_raw[chunk] = tile("q_raw%d" % chunk, [P, PACK, HALF], F32)
+            nc.sync.dma_start(out=q_raw[chunk][:], in_=q_src[P * pair : P * (pair + 1), :, HALF * half : HALF * (half + 1)])
 
         def load_mask(half):
-            m_raw[half] = sbt("m_raw%d" % half, [P, PACK, 2 * QB], F32)
-            nc.sync.dma_start(out=m_raw[half][:], in_=m_src[:, :, 2 * QB * half : 2 * QB * (half + 1)])
+            mask_raw[half] = tile("mask_raw%d" % half, [P, PACK, HALF], F32)
+            nc.sync.dma_start(out=mask_raw[half][:], in_=mask_src[:, :, HALF * half : HALF * (half + 1)])
+
+        def by_query_block(x, pair):
+            return x[2 * pair : 2 * pair + 2].rearrange("h (c p) e -> p (h c) e", p=P)
 
         def load_og(pair):
-            og_raw[pair] = sbt("og_raw%d" % pair, [P, 2 * 4, E], F32)
-            nc.sync.dma_start(out=og_raw[pair][:], in_=og[2 * pair : 2 * pair + 2].rearrange("h (c p) e -> p (h c) e", p=P))
+            og_raw[pair] = tile("og_raw%d" % pair, [P, 8, VALUES], F32)
+            nc.sync.dma_start(out=og_raw[pair][:], in_=by_query_block(og, pair))
 
-        t_sb = sbt("t_sb", [P, PACK], F32)
-        v_raw = sbt("v_raw", [P, PACK, E], F32)
+        t_sb = tile("t_sb", [P, PACK], F32)
+        v_raw = tile("v_raw", [P, PACK, VALUES], F32)
+        load_k(0)
+        load_k(1)
         load_q(0)
-        nc.sync.dma_start(out=t_sb[:], in_=t.rearrange("(p r) o -> p (r o)", r=PACK))
+        nc.sync.dma_start(out=t_sb[:], in_=t.rearrange("(s r) o -> s (r o)", r=PACK))
         load_mask(0)
 
-        def later_loads():
-            load_q(1)
-            load_q(2)
-            load_mask(1)
-            load_q(3)
-            nc.sync.dma_start(out=v_raw[:], in_=v[0].rearrange("(p r) e -> p r e", r=PACK))
-            load_og(0)
-            load_og(1)
+        k_mx = [tile("k_mx%d" % g, [P, TOKENS + TOKENS // PACK], U32) for g in range(2)]
+        k_codes = [k_mx[g][:, 0:TOKENS] for g in range(2)]
+        k_scales = [k_mx[g][:, TOKENS:].bitcast(U8) for g in range(2)]
+        nc.vector.memset(k_mx[0][0:TILE_ROWS, TOKENS:], 0)
 
-        k_tiles = [sbt("k_mx%d" % g, [P, N + N // 4], U32) for g in range(2)]
-        nc.vector.memset(k_tiles[0][0:ROWS, N:], 0)
-
-        zero_in = sbt("zero_in", [P, 1], F32)
-        zero = sbt("zero", [P, 1], F32)
+        zero_in = tile("zero_in", [P, 1], F32)
+        zero = tile("zero", [P, 1], F32)
         nc.vector.memset(zero_in[:], 0.0)
         nc.scalar.activation(out=zero[:], in_=zero_in[:], func=ACT.Silu)
 
+        def on_vector(dst, src):
+            nc.vector.tensor_copy(out=dst, in_=src)
+
+        def on_scalar(dst, src):
+            nc.scalar.copy(out=dst, in_=src)
+
         def quantize(name, src, words):
-            codes = sbt(name + "_c", [P, words], U32)
-            scales = sbt(name + "_s", [P, words], U8)
+            codes = tile(name + "_codes", [P, words], U32)
+            scales = tile(name + "_scales", [P, words], U8)
             nc.vector.quantize_mx(out=codes[:].bitcast(FP8X4), scales=scales[:], in_=src)
             return codes, scales
 
-        def copy_on(engine, dst, src):
-            if engine == "vector":
-                nc.vector.tensor_copy(out=dst, in_=src)
-            else:
-                nc.scalar.copy(out=dst, in_=src)
+        def matmul(dst, stationary, moving):
+            nc.tensor.matmul_mx(
+                out=dst,
+                lhsT=stationary[0].bitcast(FP8X4),
+                lhsT_scale=stationary[1],
+                rhs=moving[0].bitcast(FP8X4),
+                rhs_scale=moving[1],
+                start=True,
+                stop=True,
+            )
 
-        k_bf, q_bf, q_mx, mt, pw, w_bf, w_mx, th = {}, {}, {}, {}, {}, {}, {}, {}
-        k_codes = [k_tiles[g][:, 0:N] for g in range(2)]
-        k_scales = [k_tiles[g][:, N:].bitcast(U8) for g in range(2)]
+        k_bf = [tile("k_bf%d" % rr, [TILE_ROWS, 2, P, PACK], BF16) for rr in range(2)]
 
-        def cast_k(a, rr, engine):
-            if rr not in k_bf:
-                k_bf[rr] = sbt("k_bf%d" % rr, [ROWS, 2, P, PACK], BF16)
+        def cast_k(a, rr, copy):
             src = k_raw[a][:].rearrange("p j (s rr r) -> p rr s j r", rr=2, r=2)[:, rr]
-            copy_on(engine, k_bf[rr][:, :, P // 2 * a : P // 2 * (a + 1), :].rearrange("p r s j -> p s j r"), src)
+            copy(k_bf[rr][:, :, P // 2 * a : P // 2 * (a + 1), :].rearrange("p r s j -> p s j r"), src)
 
-        def quant_k(r):
+        def quantize_k(r):
             cols = slice(P * r, P * (r + 1))
             nc.vector.quantize_mx(
-                out=k_codes[0][0:ROWS, cols].bitcast(FP8X4),
-                scales=k_scales[0][0:ROWS, cols],
+                out=k_codes[0][0:TILE_ROWS, cols].bitcast(FP8X4),
+                scales=k_scales[0][0:TILE_ROWS, cols],
                 in_=k_bf[r // 2][:, r % 2].rearrange("p s j -> p (s j)"),
             )
 
-        def copy_k():
-            nc.sync.dma_start(out=k_tiles[1][ROWS:P, :].bitcast(I32), in_=k_tiles[0][0:ROWS, :].bitcast(I32))
+        def interleaved(dst, src):
+            return dst.rearrange("p (m i) j -> p m j i", i=RUN), src.rearrange("p j (m i) -> p m j i", i=RUN)
 
-        def cast_q(i, c0, c1, engine):
-            key = (i, c0) if i == 0 else i
-            if key not in q_bf:
-                q_bf[key] = sbt("q_bf%d_%d" % (i, c0), [P, QB * (1 if i == 0 else 2), PACK], BF16)
-            dst = q_bf[key][:] if i == 0 else q_bf[key][:, QB * c0 : QB * c1, :]
-            src = q_raw[i][:, :, QB * c0 : QB * c1].rearrange("p j (m i) -> p m j i", i=RUN)
-            copy_on(engine, dst.rearrange("p (m i) j -> p m j i", i=RUN), src)
+        q_bf = [tile("q_bf%d" % chunk, [P, HALF, PACK], BF16) for chunk in range(4)]
+        q_mx = {}
 
-        def quant_q_block(c):
-            codes, scales = quantize("q0_%d" % c, q_bf[0, c][:].rearrange("p n j -> p (n j)"), QB)
-            q_mx[0, c] = (codes[:], scales[:])
+        def cast_q(chunk, blocks, copy):
+            cols = slice(BLOCK * blocks.start, BLOCK * blocks.stop)
+            copy(*interleaved(q_bf[chunk][:, cols, :], q_raw[chunk][:, :, cols]))
 
-        def quant_q(i):
-            codes, scales = quantize("q%d" % i, q_bf[i][:].rearrange("p n j -> p (n j)"), 2 * QB)
-            for c in range(2):
-                q_mx[i, c] = (codes[:, QB * c : QB * (c + 1)], scales[:, QB * c : QB * (c + 1)])
+        def quantize_q(chunk, blocks):
+            src = q_bf[chunk][:, BLOCK * blocks.start : BLOCK * blocks.stop, :].rearrange("p n j -> p (n j)")
+            codes, scales = quantize("q%d_%d" % (chunk, blocks.start), src, BLOCK * len(blocks))
+            for n, c in enumerate(blocks):
+                q_mx[chunk, c] = (codes[:, BLOCK * n : BLOCK * (n + 1)], scales[:, BLOCK * n : BLOCK * (n + 1)])
 
-        def make_mt(half):
-            mt[half] = sbt("mt%d" % half, [P, PACK, 2 * QB], F32)
+        mask_t = {}
+
+        def mask_times_t(half):
+            mask_t[half] = tile("mask_t%d" % half, [P, PACK, HALF], F32)
             for r in range(PACK):
                 nc.vector.tensor_scalar(
-                    out=mt[half][:, r, :], in0=m_raw[half][:, r, :], scalar1=t_sb[:, r : r + 1], scalar2=None, op0=ALU.mult
+                    out=mask_t[half][:, r, :], in0=mask_raw[half][:, r, :], scalar1=t_sb[:, r : r + 1], scalar2=None, op0=ALU.mult
                 )
 
-        def bank(u, c):
-            return score_banks[u % 2][(2 * (u // 2) + c) % 3]
+        def score_bank(u, c):
+            return score_banks[u % 2][(2 * (u // 2) + c) % SCORE_BANKS]
 
         def scores(u):
             g = u % 2
-            rows = slice(ROWS * g, ROWS * (g + 1))
+            rows = slice(TILE_ROWS * g, TILE_ROWS * (g + 1))
             for c in range(2):
-                qc, qs = q_mx[u // 2, c]
+                q_codes, q_scales = q_mx[u // 2, c]
                 for r in range(PACK):
                     cols = slice(P * r, P * (r + 1))
-                    nc.tensor.matmul_mx(
-                        out=bank(u, c)[:, r, :],
-                        lhsT=k_codes[g][rows, cols].bitcast(FP8X4),
-                        lhsT_scale=k_scales[g][rows, cols],
-                        rhs=qc[rows, :].bitcast(FP8X4),
-                        rhs_scale=qs[rows, :],
-                        start=True,
-                        stop=True,
+                    matmul(
+                        score_bank(u, c)[:, r, :],
+                        (k_codes[g][rows, cols], k_scales[g][rows, cols]),
+                        (q_codes[rows, :], q_scales[rows, :]),
                     )
 
+        p_sb = [tile("p%d" % u, [P, HALF // RUN, PACK, RUN], F32) for u in range(8)]
+        w_bf = [tile("w%d" % u, [P, HALF, PACK], BF16) for u in range(8)]
+        w_mx = {}
+
         def silu(u, c):
-            if u not in pw:
-                pw[u] = sbt("p%d" % u, [P, 2 * QB // RUN, PACK, RUN], F32)
             nc.scalar.activation(
-                out=pw[u][:, QB // RUN * c : QB // RUN * (c + 1)],
-                in_=bank(u, c)[:].rearrange("p r (m i) -> p m r i", i=RUN),
+                out=p_sb[u][:, BLOCK // RUN * c : BLOCK // RUN * (c + 1)],
+                in_=score_bank(u, c)[:].rearrange("p r (m i) -> p m r i", i=RUN),
                 func=ACT.Silu,
                 bias=zero[:],
             )
 
-        def mult(u, c0, c1):
-            if u not in w_bf:
-                w_bf[u] = sbt("w%d" % u, [P, 2 * QB * PACK], BF16)
-            nc.vector.tensor_tensor(
-                out=w_bf[u][:, QB * PACK * c0 : QB * PACK * c1].rearrange("p (m i r) -> p m r i", i=RUN, r=PACK),
-                in0=pw[u][:, QB // RUN * c0 : QB // RUN * c1],
-                in1=mt[(u // 2) % 2][:, :, QB * c0 : QB * c1].rearrange("p r (m i) -> p m r i", i=RUN),
-                op=ALU.mult,
-            )
+        def weigh(u, blocks):
+            cols = slice(BLOCK * blocks.start, BLOCK * blocks.stop)
+            dst, factor = interleaved(w_bf[u][:, cols, :], mask_t[(u // 2) % 2][:, :, cols])
+            nc.vector.tensor_tensor(out=dst, in0=p_sb[u][:, cols.start // RUN : cols.stop // RUN], in1=factor, op=ALU.mult)
 
-        def quant_w(u, c0, c1):
-            codes, scales = quantize("wq%d_%d" % (u, c0), w_bf[u][:, QB * PACK * c0 : QB * PACK * c1], QB * (c1 - c0))
-            for c in range(c0, c1):
-                cols = slice(QB * (c - c0), QB * (c - c0 + 1))
-                w_mx[u, c] = (codes[:, cols], scales[:, cols])
+        def quantize_w(u, blocks):
+            src = w_bf[u][:, BLOCK * blocks.start : BLOCK * blocks.stop, :].rearrange("p q r -> p (q r)")
+            codes, scales = quantize("w%d_%d" % (u, blocks.start), src, BLOCK * len(blocks))
+            for n, c in enumerate(blocks):
+                w_mx[u, c] = (codes[:, BLOCK * n : BLOCK * (n + 1)], scales[:, BLOCK * n : BLOCK * (n + 1)])
 
-        v_bf = sbt("v_bf", [P, E, PACK], BF16)
+        v_bf = tile("v_bf", [P, VALUES, PACK], BF16)
         v_mx = []
 
         def cast_v():
-            nc.scalar.activation(
-                out=v_bf[:].rearrange("p (m i) r -> p m r i", i=RUN),
-                in_=v_raw[:].rearrange("p r (m i) -> p m r i", i=RUN),
-                func=ACT.Copy,
-                scale=1.0 / 32.0,
-            )
+            dst, src = interleaved(v_bf[:], v_raw[:])
+            nc.vector.tensor_scalar(out=dst, in0=src, scalar1=1.0 / 32.0, scalar2=None, op0=ALU.mult)
 
-        def quant_v():
-            v_mx.extend(quantize("v", v_bf[:].rearrange("p e r -> p (e r)"), E))
+        def quantize_v():
+            codes, scales = quantize("v", v_bf[:].rearrange("p e r -> p (e r)"), VALUES)
+            v_mx.extend([codes[:], scales[:]])
 
-        y_place = [(0, 0), (1, 1), (1, 0), (0, 1), (0, 0), (1, 1), (1, 0), (0, 1)]
+        y_place = [(0, 0), (0, 1), (1, 0), (1, 1), (0, 0), (1, 1), (1, 0), (0, 1)]
 
-        def pv(u, blocks=(0, 1)):
+        def product(u, blocks):
             b, slot = y_place[u]
             for c in blocks:
-                wc, ws = w_mx[u, c]
-                nc.tensor.matmul_mx(
-                    out=y_banks[b][:, slot, c, :],
-                    lhsT=wc.bitcast(FP8X4),
-                    lhsT_scale=ws,
-                    rhs=v_mx[0][:].bitcast(FP8X4),
-                    rhs_scale=v_mx[1][:],
-                    start=True,
-                    stop=True,
-                )
+                matmul(y_banks[b][:, slot, c, :], w_mx[u, c], v_mx)
 
-        def quarters(ap, which):
-            return ap.rearrange("p (a c) e -> p a (c e)", c=2)[:, which, :]
+        def quarters(x, which):
+            return x.rearrange("p (a c) e -> p a (c e)", c=2)[:, which.start : which.stop : which.step, :]
+
+        tanh_sb = [tile("tanh%d" % pair, [P, 8, VALUES], F32) for pair in range(2)]
 
         def tanh(pair, which):
-            if pair not in th:
-                th[pair] = sbt("th%d" % pair, [P, 8, E], F32)
-            nc.scalar.activation(out=quarters(th[pair][:], which), in_=quarters(og_raw[pair][:], which), func=ACT.Tanh, scale=0.5)
+            nc.scalar.activation(
+                out=quarters(tanh_sb[pair][:], which), in_=quarters(og_raw[pair][:], which), func=ACT.Tanh, scale=0.5
+            )
 
         def gate(pair, which, b, slots):
-            n = len(range(4)[which])
-            res = sbt("res%d_%d" % (pair, which.start), [P, n, 2 * E], F32)
+            result = tile("result%d_%d" % (pair, which.start), [P, len(which), 2 * VALUES], F32)
             nc.vector.scalar_tensor_tensor(
-                out=res[:],
-                in0=quarters(th[pair][:], which),
+                out=result[:],
+                in0=quarters(tanh_sb[pair][:], which),
                 scalar=1.0,
-                in1=y_banks[b][:].rearrange("p a c e -> p a (c e)")[:, slots, :],
+                in1=y_banks[b][:].rearrange("p a c e -> p a (c e)")[:, slots.start : slots.stop, :],
                 op0=ALU.add,
                 op1=ALU.mult,
             )
-            rows = out[2 * pair : 2 * pair + 2].rearrange("h (c p) e -> p (h c) e", p=P)
-            if which.step == 1:
-                nc.sync.dma_start(out=rows[:, 2 * which.start : 2 * which.stop, :], in_=res[:].rearrange("p a (c e) -> p (a c) e", c=2))
-            else:
-                for i, a in enumerate(range(4)[which]):
-                    nc.sync.dma_start(out=rows[:, 2 * a : 2 * a + 2, :], in_=res[:, i, :].rearrange("p (c e) -> p c e", c=2))
+            length = len(which) if which.step == 1 else 1
+            for n in range(0, len(which), length):
+                nc.sync.dma_start(
+                    out=by_query_block(out, pair)[:, 2 * which[n] : 2 * (which[n] + length), :],
+                    in_=result[:, n : n + length, :].rearrange("p a (c e) -> p (a c) e", c=2),
+                )
 
-        outer, inner, first, last = slice(0, 4, 3), slice(1, 3, 1), slice(0, 1, 1), slice(3, 4, 1)
+        first, second, both = range(0, 1), range(1, 2), range(0, 2)
 
-        cast_k(0, 0, "vector")
-        cast_k(0, 1, "vector")
-        cast_k(1, 0, "vector")
-        cast_k(1, 1, "scalar")
+        cast_k(0, 0, on_vector)
+        cast_k(0, 1, on_vector)
+        cast_k(1, 0, on_vector)
+        cast_k(1, 1, on_scalar)
         for r in range(PACK):
-            quant_k(r)
-        cast_q(0, 0, 1, "vector")
-        cast_q(0, 1, 2, "scalar")
-        copy_k()
-        later_loads()
-        quant_q_block(0)
-        quant_q_block(1)
+            quantize_k(r)
+        cast_q(0, first, on_vector)
+        cast_q(0, second, on_scalar)
+        nc.sync.dma_start(out=k_mx[1][TILE_ROWS:P, :].bitcast(I32), in_=k_mx[0][0:TILE_ROWS, :].bitcast(I32))
+        load_q(1)
+        load_q(2)
+        load_mask(1)
+        load_q(3)
+        nc.sync.dma_start(out=v_raw[:], in_=v[0].rearrange("(s r) e -> s r e", r=PACK))
+        load_og(0)
+        load_og(1)
+        quantize_q(0, first)
+        quantize_q(0, second)
         scores(0)
         scores(1)
-        make_mt(0)
+        mask_times_t(0)
+
         silu(0, 0)
         silu(0, 1)
         silu(1, 0)
-        cast_q(1, 0, 1, "scalar")
-        mult(0, 0, 1)
-        mult(0, 1, 2)
-        cast_q(1, 1, 2, "vector")
+        cast_q(1, first, on_scalar)
+        weigh(0, first)
+        weigh(0, second)
+        cast_q(1, second, on_vector)
+        quantize_w(0, both)
+        quantize_q(1, both)
         silu(1, 1)
-        quant_w(0, 0, 2)
-        quant_q(1)
         scores(2)
         scores(3)
-        cast_q(2, 0, 2, "scalar")
-        mult(1, 0, 2)
-        make_mt(1)
-        quant_w(1, 0, 2)
-        quant_q(2)
-        silu(2, 0)
-        silu(2, 1)
-        scores(4)
-        silu(3, 0)
-        silu(3, 1)
-        scores(5)
-        mult(2, 0, 2)
-        cast_q(3, 0, 2, "scalar")
-        mult(3, 0, 2)
-        quant_w(2, 0, 2)
-        quant_q(3)
-        quant_w(3, 0, 2)
+        cast_q(2, both, on_scalar)
+
+        weigh(1, both)
+        mask_times_t(1)
+        quantize_w(1, both)
+        quantize_q(2, both)
+        for u in (2, 3):
+            silu(u, 0)
+            silu(u, 1)
+            scores(u + 2)
+        cast_q(3, both, on_scalar)
+
+        weigh(2, both)
+        cast_v()
+        quantize_w(2, both)
+
+        weigh(3, both)
+        quantize_v()
+        quantize_q(3, both)
+        quantize_w(3, both)
+        product(0, both)
+        product(1, both)
+
         silu(4, 0)
         silu(4, 1)
+        tanh(0, range(0, 4, 2))
         scores(6)
-        cast_v()
-        mult(4, 0, 2)
-        quant_v()
-        quant_w(4, 0, 2)
-        for u in range(4):
-            pv(u)
+        product(2, both)
+        product(3, both)
+        weigh(4, both)
+        gate(0, range(0, 4, 2), 0, both)
+        quantize_w(4, both)
+
         silu(5, 0)
         silu(5, 1)
-        tanh(0, outer)
+        tanh(0, range(1, 4, 2))
         scores(7)
-        mult(5, 0, 2)
-        gate(0, outer, 0, slice(0, 2))
-        pv(4)
-        quant_w(5, 0, 2)
-        tanh(0, inner)
+        product(4, both)
+        weigh(5, both)
+        gate(0, range(1, 4, 2), 1, both)
+        quantize_w(5, both)
+        product(5, both)
+
         silu(6, 0)
         silu(6, 1)
-        tanh(1, first)
-        gate(0, inner, 1, slice(0, 2))
-        pv(5)
-        mult(6, 0, 2)
-        gate(1, first, 0, slice(0, 1))
-        quant_w(6, 0, 2)
-        pv(6)
+        tanh(1, range(0, 1))
+        weigh(6, both)
+        gate(1, range(0, 1), 0, first)
+        quantize_w(6, both)
+        product(6, both)
+
         silu(7, 0)
         silu(7, 1)
-        tanh(1, slice(1, 4, 1))
-        mult(7, 0, 1)
-        mult(7, 1, 2)
-        quant_w(7, 0, 1)
-        pv(7, (0,))
-        quant_w(7, 1, 2)
-        pv(7, (1,))
-        gate(1, inner, 1, slice(0, 2))
-        gate(1, last, 0, slice(1, 2))
+        tanh(1, range(1, 4))
+        weigh(7, first)
+        weigh(7, second)
+        for blocks in (first, second):
+            quantize_w(7, blocks)
+            product(7, blocks)
+        gate(1, range(1, 3), 1, both)
+        gate(1, range(3, 4), 0, second)

from contextlib import ExitStack

import concourse.mybir as mybir

HEADS, FEATURES, QUERIES, TOKENS, VALUES = 4, 256, 512, 512, 128
FLOPS = 2 * HEADS * TOKENS * QUERIES * (FEATURES + VALUES)

F32 = mybir.dt.float32
BF16 = mybir.dt.bfloat16
I32 = mybir.dt.int32
U32 = mybir.dt.uint32
U8 = mybir.dt.uint8
FP8X4 = mybir.dt.float8_e4m3fn_x4
ACT = mybir.ActivationFunctionType
ALU = mybir.AluOpType

P = 128
PACK = 4
TILE_ROWS = FEATURES // PACK
BLOCK = 128
HALF = 2 * BLOCK
RUN = 2
SCORE_BANKS = 3


def tile_rows_a_silu_mask_gate_kernel(tc, qT, kT, t, v, mask, og, out):
    nc = tc.nc
    with ExitStack() as ctx:
        sbuf = ctx.enter_context(tc.tile_pool(name="sbuf", bufs=1))
        psum = ctx.enter_context(tc.psum_pool(name="psum", bufs=1))
        ctx.enter_context(tc.manual_schedule())

        def tile(name, shape, dtype):
            return sbuf.tile(shape, dtype, name=name, align_bytes=64)

        score_banks = [
            [psum.tile([P, PACK, BLOCK], F32, name="s%d_%d" % (g, b)) for b in range(SCORE_BANKS)] for g in range(2)
        ]
        y_banks = [psum.tile([P, 2, 2, VALUES], F32, name="y%d" % b) for b in range(2)]

        k_src = kT[0].rearrange("(p j) n -> p j n", j=PACK)
        q_src = qT.rearrange("h (p j) n -> (h p) j n", j=PACK)
        mask_src = mask.rearrange("(s r) q -> s r q", r=PACK)
        k_raw, q_raw, mask_raw, og_raw = {}, {}, {}, {}

        def load_k(a):
            k_raw[a] = tile("k_raw%d" % a, [TILE_ROWS, PACK, TOKENS // 2], F32)
            nc.sync.dma_start(out=k_raw[a][:], in_=k_src[:, :, TOKENS // 2 * a : TOKENS // 2 * (a + 1)])

        def load_q(chunk):
            pair, half = divmod(chunk, 2)
            q_raw[chunk] = tile("q_raw%d" % chunk, [P, PACK, HALF], F32)
            nc.sync.dma_start(out=q_raw[chunk][:], in_=q_src[P * pair : P * (pair + 1), :, HALF * half : HALF * (half + 1)])

        def load_mask(half):
            mask_raw[half] = tile("mask_raw%d" % half, [P, PACK, HALF], F32)
            nc.sync.dma_start(out=mask_raw[half][:], in_=mask_src[:, :, HALF * half : HALF * (half + 1)])

        def by_query_block(x, pair):
            return x[2 * pair : 2 * pair + 2].rearrange("h (c p) e -> p (h c) e", p=P)

        def load_og(pair):
            og_raw[pair] = tile("og_raw%d" % pair, [P, 8, VALUES], F32)
            nc.sync.dma_start(out=og_raw[pair][:], in_=by_query_block(og, pair))

        t_sb = tile("t_sb", [P, PACK], F32)
        v_raw = tile("v_raw", [P, PACK, VALUES], F32)
        load_k(0)
        load_k(1)
        load_q(0)
        nc.sync.dma_start(out=t_sb[:], in_=t.rearrange("(s r) o -> s (r o)", r=PACK))
        load_mask(0)

        k_mx = [tile("k_mx%d" % g, [P, TOKENS + TOKENS // PACK], U32) for g in range(2)]
        k_codes = [k_mx[g][:, 0:TOKENS] for g in range(2)]
        k_scales = [k_mx[g][:, TOKENS:].bitcast(U8) for g in range(2)]
        nc.vector.memset(k_mx[0][0:TILE_ROWS, TOKENS:], 0)

        zero_in = tile("zero_in", [P, 1], F32)
        zero = tile("zero", [P, 1], F32)
        nc.vector.memset(zero_in[:], 0.0)
        nc.scalar.activation(out=zero[:], in_=zero_in[:], func=ACT.Silu)

        def on_vector(dst, src):
            nc.vector.tensor_copy(out=dst, in_=src)

        def on_scalar(dst, src):
            nc.scalar.copy(out=dst, in_=src)

        def quantize(name, src, words):
            codes = tile(name + "_codes", [P, words], U32)
            scales = tile(name + "_scales", [P, words], U8)
            nc.vector.quantize_mx(out=codes[:].bitcast(FP8X4), scales=scales[:], in_=src)
            return codes, scales

        def matmul(dst, stationary, moving):
            nc.tensor.matmul_mx(
                out=dst,
                lhsT=stationary[0].bitcast(FP8X4),
                lhsT_scale=stationary[1],
                rhs=moving[0].bitcast(FP8X4),
                rhs_scale=moving[1],
                start=True,
                stop=True,
            )

        k_bf = [tile("k_bf%d" % rr, [TILE_ROWS, 2, P, PACK], BF16) for rr in range(2)]

        def cast_k(a, rr, copy):
            src = k_raw[a][:].rearrange("p j (s rr r) -> p rr s j r", rr=2, r=2)[:, rr]
            copy(k_bf[rr][:, :, P // 2 * a : P // 2 * (a + 1), :].rearrange("p r s j -> p s j r"), src)

        def quantize_k(r):
            cols = slice(P * r, P * (r + 1))
            nc.vector.quantize_mx(
                out=k_codes[0][0:TILE_ROWS, cols].bitcast(FP8X4),
                scales=k_scales[0][0:TILE_ROWS, cols],
                in_=k_bf[r // 2][:, r % 2].rearrange("p s j -> p (s j)"),
            )

        def interleaved(dst, src):
            return dst.rearrange("p (m i) j -> p m j i", i=RUN), src.rearrange("p j (m i) -> p m j i", i=RUN)

        q_bf = [tile("q_bf%d" % chunk, [P, HALF, PACK], BF16) for chunk in range(4)]
        q_mx = {}

        def cast_q(chunk, blocks, copy):
            cols = slice(BLOCK * blocks.start, BLOCK * blocks.stop)
            copy(*interleaved(q_bf[chunk][:, cols, :], q_raw[chunk][:, :, cols]))

        def quantize_q(chunk, blocks):
            src = q_bf[chunk][:, BLOCK * blocks.start : BLOCK * blocks.stop, :].rearrange("p n j -> p (n j)")
            codes, scales = quantize("q%d_%d" % (chunk, blocks.start), src, BLOCK * len(blocks))
            for n, c in enumerate(blocks):
                q_mx[chunk, c] = (codes[:, BLOCK * n : BLOCK * (n + 1)], scales[:, BLOCK * n : BLOCK * (n + 1)])

        mask_t = {}

        def mask_times_t(half):
            mask_t[half] = tile("mask_t%d" % half, [P, PACK, HALF], F32)
            for r in range(PACK):
                nc.vector.tensor_scalar(
                    out=mask_t[half][:, r, :], in0=mask_raw[half][:, r, :], scalar1=t_sb[:, r : r + 1], scalar2=None, op0=ALU.mult
                )

        def score_bank(u, c):
            return score_banks[u % 2][(2 * (u // 2) + c) % SCORE_BANKS]

        def scores(u):
            g = u % 2
            rows = slice(TILE_ROWS * g, TILE_ROWS * (g + 1))
            for c in range(2):
                q_codes, q_scales = q_mx[u // 2, c]
                for r in range(PACK):
                    cols = slice(P * r, P * (r + 1))
                    matmul(
                        score_bank(u, c)[:, r, :],
                        (k_codes[g][rows, cols], k_scales[g][rows, cols]),
                        (q_codes[rows, :], q_scales[rows, :]),
                    )

        p_sb = [tile("p%d" % u, [P, HALF // RUN, PACK, RUN], F32) for u in range(8)]
        w_bf = [tile("w%d" % u, [P, HALF, PACK], BF16) for u in range(8)]
        w_mx = {}

        def silu(u, c):
            nc.scalar.activation(
                out=p_sb[u][:, BLOCK // RUN * c : BLOCK // RUN * (c + 1)],
                in_=score_bank(u, c)[:].rearrange("p r (m i) -> p m r i", i=RUN),
                func=ACT.Silu,
                bias=zero[:],
            )

        def weigh(u, blocks):
            cols = slice(BLOCK * blocks.start, BLOCK * blocks.stop)
            dst, factor = interleaved(w_bf[u][:, cols, :], mask_t[(u // 2) % 2][:, :, cols])
            nc.vector.tensor_tensor(out=dst, in0=p_sb[u][:, cols.start // RUN : cols.stop // RUN], in1=factor, op=ALU.mult)

        def quantize_w(u, blocks):
            src = w_bf[u][:, BLOCK * blocks.start : BLOCK * blocks.stop, :].rearrange("p q r -> p (q r)")
            codes, scales = quantize("w%d_%d" % (u, blocks.start), src, BLOCK * len(blocks))
            for n, c in enumerate(blocks):
                w_mx[u, c] = (codes[:, BLOCK * n : BLOCK * (n + 1)], scales[:, BLOCK * n : BLOCK * (n + 1)])

        v_bf = tile("v_bf", [P, VALUES, PACK], BF16)
        v_mx = []

        def cast_v():
            dst, src = interleaved(v_bf[:], v_raw[:])
            nc.vector.tensor_scalar(out=dst, in0=src, scalar1=1.0 / 32.0, scalar2=None, op0=ALU.mult)

        def quantize_v():
            codes, scales = quantize("v", v_bf[:].rearrange("p e r -> p (e r)"), VALUES)
            v_mx.extend([codes[:], scales[:]])

        y_place = [(0, 0), (0, 1), (1, 0), (1, 1), (0, 0), (1, 1), (1, 0), (0, 1)]

        def product(u, blocks):
            b, slot = y_place[u]
            for c in blocks:
                matmul(y_banks[b][:, slot, c, :], w_mx[u, c], v_mx)

        def quarters(x, which):
            return x.rearrange("p (a c) e -> p a (c e)", c=2)[:, which.start : which.stop : which.step, :]

        tanh_sb = [tile("tanh%d" % pair, [P, 8, VALUES], F32) for pair in range(2)]

        def tanh(pair, which):
            nc.scalar.activation(
                out=quarters(tanh_sb[pair][:], which), in_=quarters(og_raw[pair][:], which), func=ACT.Tanh, scale=0.5
            )

        def gate(pair, which, b, slots):
            result = tile("result%d_%d" % (pair, which.start), [P, len(which), 2 * VALUES], F32)
            nc.vector.scalar_tensor_tensor(
                out=result[:],
                in0=quarters(tanh_sb[pair][:], which),
                scalar=1.0,
                in1=y_banks[b][:].rearrange("p a c e -> p a (c e)")[:, slots.start : slots.stop, :],
                op0=ALU.add,
                op1=ALU.mult,
            )
            length = len(which) if which.step == 1 else 1
            for n in range(0, len(which), length):
                nc.sync.dma_start(
                    out=by_query_block(out, pair)[:, 2 * which[n] : 2 * (which[n] + length), :],
                    in_=result[:, n : n + length, :].rearrange("p a (c e) -> p (a c) e", c=2),
                )

        first, second, both = range(0, 1), range(1, 2), range(0, 2)

        cast_k(0, 0, on_vector)
        cast_k(0, 1, on_vector)
        cast_k(1, 0, on_vector)
        cast_k(1, 1, on_scalar)
        for r in range(PACK):
            quantize_k(r)
        cast_q(0, first, on_vector)
        cast_q(0, second, on_scalar)
        nc.sync.dma_start(out=k_mx[1][TILE_ROWS:P, :].bitcast(I32), in_=k_mx[0][0:TILE_ROWS, :].bitcast(I32))
        load_q(1)
        load_q(2)
        load_mask(1)
        load_q(3)
        nc.sync.dma_start(out=v_raw[:], in_=v[0].rearrange("(s r) e -> s r e", r=PACK))
        load_og(0)
        load_og(1)
        quantize_q(0, first)
        quantize_q(0, second)
        scores(0)
        scores(1)
        mask_times_t(0)

        silu(0, 0)
        silu(0, 1)
        silu(1, 0)
        cast_q(1, first, on_scalar)
        weigh(0, first)
        weigh(0, second)
        cast_q(1, second, on_vector)
        quantize_w(0, both)
        quantize_q(1, both)
        silu(1, 1)
        scores(2)
        scores(3)
        cast_q(2, both, on_scalar)

        weigh(1, both)
        mask_times_t(1)
        quantize_w(1, both)
        quantize_q(2, both)
        for u in (2, 3):
            silu(u, 0)
            silu(u, 1)
            scores(u + 2)
        cast_q(3, both, on_scalar)

        weigh(2, both)
        cast_v()
        quantize_w(2, both)

        weigh(3, both)
        quantize_v()
        quantize_q(3, both)
        quantize_w(3, both)
        product(0, both)
        product(1, both)

        silu(4, 0)
        silu(4, 1)
        tanh(0, range(0, 4, 2))
        scores(6)
        product(2, both)
        product(3, both)
        weigh(4, both)
        gate(0, range(0, 4, 2), 0, both)
        quantize_w(4, both)

        silu(5, 0)
        silu(5, 1)
        tanh(0, range(1, 4, 2))
        scores(7)
        product(4, both)
        weigh(5, both)
        gate(0, range(1, 4, 2), 1, both)
        quantize_w(5, both)
        product(5, both)

        silu(6, 0)
        silu(6, 1)
        tanh(1, range(0, 1))
        weigh(6, both)
        gate(1, range(0, 1), 0, first)
        quantize_w(6, both)
        product(6, both)

        silu(7, 0)
        silu(7, 1)
        tanh(1, range(1, 4))
        weigh(7, first)
        weigh(7, second)
        for blocks in (first, second):
            quantize_w(7, blocks)
            product(7, blocks)
        gate(1, range(1, 3), 1, both)
        gate(1, range(3, 4), 0, second)
